import numpy as np
import ml_dtypes


def mxq(x, axis, fmt="e4m3"):
    dtype, down = {"e4m3": (ml_dtypes.float8_e4m3fn, 7), "e5m2": (ml_dtypes.float8_e5m2, 14)}[fmt]
    v = np.moveaxis(np.asarray(x, np.float32).astype(ml_dtypes.bfloat16).astype(np.float64), axis, -1)
    blocks = v.reshape(v.shape[:-1] + (-1, 32))
    amax = np.abs(blocks).max(-1, keepdims=True)
    byte = np.maximum(np.where(amax > 0, np.frexp(amax)[1] - 1 + 127, 0) - down, 1)
    scale = np.exp2(byte - 127.0)
    codes = (blocks / scale).astype(np.float32).astype(dtype).astype(np.float64)
    return np.moveaxis((codes * scale).reshape(v.shape), -1, axis)


WIDE = False


def mx_kscale(k):
    if not WIDE:
        return np.ones(k)
    levels = np.array([10, -10, 5, -5, 0])
    if k % 512:
        return np.exp2(np.random.permutation(np.resize(levels, k // 32))).repeat(32)
    a = np.empty((k // 512, 16))
    for p in range(k // 512):
        a[p, :8] = np.random.permutation(np.resize(levels, 8))
        for g in range(8):
            far = levels[np.abs(levels - a[p, g]) >= 10]
            a[p, g + 8] = far[np.random.randint(len(far))]
    return np.exp2(a.ravel()).repeat(32)


def f64(x):
    return np.asarray(x).astype(np.float64)


def striped(idx):
    return np.tile(np.asarray(idx).reshape(-1, 16).T, (8, 1)).astype(np.uint16)


def unstriped(offs):
    return offs[:16].T.reshape(-1).astype(np.int64)


E2M1 = np.array([0.0, 0.5, 1.0, 1.5, 2.0, 3.0, 4.0, 6.0, -0.0, -0.5, -1.0, -1.5, -2.0, -3.0, -4.0, -6.0])


def pack_weight(w, fmt):
    k, n = w.shape
    w = f64(np.asarray(w, np.float32).astype(ml_dtypes.bfloat16)).reshape(k // 32, 32, n)
    amax = np.abs(w).max(1)
    if fmt == "e4m3":
        byte = np.frexp(amax)[1] - 1 + 127 - 7
    else:
        mant, ex = np.frexp(amax / 6.0)
        byte = np.where(mant > 0.5, ex, ex - 1) + 127
    byte = np.clip(np.where(amax > 0, byte, 1), 1, 254)
    scaled = (w * np.exp2(127.0 - byte)[:, None, :]).reshape(k, n).astype(np.float32)
    by_word = np.ascontiguousarray(scaled.reshape(k // 512, 128, 4, n).transpose(0, 1, 3, 2))
    if fmt == "e4m3":
        words = by_word.astype(ml_dtypes.float8_e4m3fn).view(np.uint8)
    else:
        c = by_word.astype(ml_dtypes.float4_e2m1fn).view(np.uint8) & 0xF
        words = (c[..., 0::2] | (c[..., 1::2] << 4)).reshape(k // 512, 128, 2 * n)
    return np.ascontiguousarray(words), np.ascontiguousarray(byte.astype(np.uint8).reshape(k // 512, 16, n))


def unpack_weight(words, scales, fmt):
    g, _, n = scales.shape
    words = np.ascontiguousarray(words).reshape(g, 128, n, -1)
    if fmt == "e4m3":
        vals = words.view(ml_dtypes.float8_e4m3fn).astype(np.float64)
    else:
        nib = np.empty((g, 128, n, 4), np.uint8)
        nib[..., 0::2] = words & 0xF
        nib[..., 1::2] = words >> 4
        vals = E2M1[nib]
    vals = vals * np.repeat(np.exp2(scales.astype(np.float64) - 127.0), 8, axis=1)[..., None]
    return vals.transpose(0, 1, 3, 2).reshape(g * 512, n)


D, T, I, Q, E = 512, 2048, 512, 128, 512


def setup_inputs():
    n = np.random.standard_normal
    idx = np.random.permutation(T)[:I]
    fd = mx_kscale(D)
    fi = mx_kscale(I)
    ti = np.ones(T)
    ti[idx] = fi
    keysp = pack_weight(n((D, T)) / fd[:, None], "e4m3")
    return {
        "query": (n((D, Q)) * 0.7 / np.sqrt(D) * fd[:, None]).astype(np.float32),
        "query2": (n((D, Q)) * 0.7 / np.sqrt(D) * fd[:, None]).astype(np.float32),
        "keys_words": keysp[0],
        "keys_scales": keysp[1],
        "xmark": np.tile(np.random.uniform(-1.0, 1.0, T), (128, 1)).astype(np.float32),
        "ymark": np.tile(np.random.uniform(-1.0, 1.0, T), (128, 1)).astype(np.float32),
        "lam": (np.random.uniform(0.5, 1.2, (Q, 1))).astype(np.float32),
        "lean": (np.random.uniform(0.2, 0.6, (Q, 1))).astype(np.float32),
        "os": (np.random.uniform(4.0, 16.0, (1, I)) * fi).astype(np.float32),
        "vals": (n((E, T)) / ti).astype(np.float32),
        "vsharp": (np.random.uniform(0.6, 1.2, (Q, 1))).astype(np.float32),
        "offs": striped(idx),
    }


def reference(query, query2, keys_words, keys_scales, xmark, ymark, lam, lean, os, vals, vsharp, offs):
    idx = unstriped(offs)
    keysu = unpack_weight(keys_words, keys_scales, "e4m3")
    queryq = mxq(f64(query), 0, "e4m3")
    keysidxg = keysu[:, idx]
    a = queryq.T @ keysidxg
    query2q = mxq(f64(query2), 0, "e4m3")
    b = query2q.T @ keysidxg
    dx = a - f64(xmark)[:1][:, idx]
    dy = b - f64(ymark)[:1][:, idx]
    s = (np.square(dx) + np.square(dy)) * f64(lam) * (-1.0)
    p = np.exp(s - np.max(s, axis=1, keepdims=True))
    r = p / np.sum(p, axis=1, keepdims=True)
    m0 = np.sum(r * s, axis=1, keepdims=True)
    w = r * ((s - m0) * f64(lean) + 1.0)
    wo1 = w * f64(os)
    wt1 = wo1.T
    vt1 = f64(vals)[:, idx].T
    wt1q = mxq(wt1, 0, "e4m3")
    vt1q = mxq(vt1, 0, "e4m3")
    o = wt1q.T @ vt1q
    oz = o * f64(vsharp)
    oe = np.exp(oz - np.max(oz, axis=1, keepdims=True))
    y = oe / np.sum(oe, axis=1, keepdims=True) * 512.0
    return y

@@ -1,0 +1,251 @@
+from contextlib import ExitStack
+
+import concourse.mybir as mybir
+from concourse.masks import make_identity
+
+D, T, I, Q, E = 512, 2048, 512, 128, 512
+FLOPS = 2 * D * I * 2 * Q + 2 * I * Q * E
+BYTES = 4 * (2 * D * Q + E * T + 2 * T + 3 * Q + I + Q * E) + D * T + 16 * T + 2 * 128 * 32
+
+F32 = mybir.dt.float32
+BF16 = mybir.dt.bfloat16
+I32 = mybir.dt.int32
+U32 = mybir.dt.uint32
+U16 = mybir.dt.uint16
+U8 = mybir.dt.uint8
+FP8X4 = mybir.dt.float8_e4m3fn_x4
+ALU = mybir.AluOpType
+ACT = mybir.ActivationFunctionType
+
+P = 128
+PACK = 4
+CHUNKS = I // P
+PLANES = E // P
+
+
+def tile_attend_maplace_leaning_readshares_kernel(
+    tc, query, query2, keys_words, keys_scales, xmark, ymark, lam, lean, slot_factor, vals, vsharp, offs, out
+):
+    nc = tc.nc
+    with ExitStack() as ctx:
+        sb = ctx.enter_context(tc.tile_pool(name="sb", bufs=1))
+        ps = ctx.enter_context(tc.psum_pool(name="ps", bufs=1))
+
+        offsets = sb.tile([P, I // 16], U16, name="offsets")
+        nc.sync.dma_start(offsets[:], offs)
+
+        key_scale_pool = sb.tile([P, T], U8, name="key_scale_pool", tag="slot_scales", align_bytes=64)
+        nc.vector.memset(key_scale_pool[:].bitcast(I32), 0)
+        for quad in range(4):
+            nc.scalar.dma_start(
+                key_scale_pool[32 * quad : 32 * quad + 4, :].bitcast(I32),
+                keys_scales[0, 4 * quad : 4 * quad + 4, :].bitcast(I32),
+            )
+        mark_pools = []
+        for axis, mark in enumerate((xmark, ymark)):
+            pool_tile = sb.tile([P, T], F32, name=f"mark_pool{axis}", tag=f"window{axis}", align_bytes=64)
+            nc.vector.memset(pool_tile[:].bitcast(I32), 0)
+            nc.scalar.dma_start(pool_tile[0:1, :], mark[0:1, :])
+            mark_pools.append(pool_tile)
+
+        q_raw = []
+        for axis, src in enumerate((query, query2)):
+            raw = sb.tile([P, PACK, Q], F32, name=f"q_raw{axis}")
+            nc.sync.dma_start(raw[:], src.rearrange("(p j) q -> p j q", j=PACK))
+            q_raw.append(raw)
+        key_word_pool = sb.tile([P, T], I32, name="key_word_pool", tag="slot_keys", align_bytes=64)
+        nc.sync.dma_start(key_word_pool[:], keys_words[0].rearrange("p n t -> p (n t)").bitcast(I32))
+
+        val_pools = {}
+
+        def load_vals(j):
+            tag = ("slot_vals", "slot_scales", "row0", "slot_keys")[j]
+            val_pools[j] = sb.tile([P, T], F32, name=f"val_pool{j}", tag=tag, align_bytes=64)
+            nc.sync.dma_start(val_pools[j][:], vals[P * j : P * (j + 1), :])
+
+        load_vals(0)
+
+        ident = sb.tile([P, P], F32, name="ident")
+        make_identity(nc, ident[:])
+
+        lam_col = sb.tile([P, 1], F32, name="lam_col")
+        lean_col = sb.tile([P, 1], F32, name="lean_col")
+        sharp_col = sb.tile([P, 1], F32, name="sharp_col")
+        os_cols = sb.tile([P, PACK], F32, name="os_cols")
+        nc.gpsimd.dma_start(lam_col[:], lam)
+        nc.gpsimd.dma_start(lean_col[:], lean)
+        nc.gpsimd.dma_start(os_cols[:], slot_factor[0].rearrange("(p t) -> p t", t=PACK))
+        nc.gpsimd.dma_start(sharp_col[:], vsharp)
+
+        q_grouped = sb.tile([P, 2, Q, PACK], BF16, name="q_grouped", align_bytes=64)
+        for axis in range(2):
+            nc.scalar.copy(q_grouped[:, axis, :, :], q_raw[axis][:].rearrange("p j q -> p q j"))
+        q_codes = sb.tile([P, 2 * Q], U32, name="q_codes", align_bytes=64)
+        q_scales = sb.tile([P, 2 * Q], U8, name="q_scales", align_bytes=64)
+
+        key_scales = sb.tile([P, I], U8, name="key_scales", align_bytes=64)
+        nc.vector.tensor_copy(key_scales[:], key_scale_pool[:].indirect(offsets[:]))
+        load_vals(1)
+        nc.vector.quantize_mx(
+            out=q_codes[:].bitcast(FP8X4), scales=q_scales[:], in_=q_grouped[:].rearrange("p a q j -> p (a q j)")
+        )
+
+        mark_cols = []
+
+        def gather_mark(axis):
+            row = sb.tile([P, I], F32, name=f"mark_row{axis}", tag=f"row{axis}", align_bytes=64)
+            nc.vector.tensor_copy(row[:], mark_pools[axis][:].indirect(offsets[:]))
+            turned = ps.tile([P, CHUNKS, P], F32, name=f"mark_turned{axis}", tag=f"turn{axis}")
+            for c in range(CHUNKS):
+                nc.tensor.transpose(turned[:, c, :], row[:, P * c : P * (c + 1)], ident[:])
+            cols = sb.tile([P, CHUNKS], F32, name=f"mark_cols{axis}")
+            nc.scalar.copy(cols[:], turned[:, :, 0])
+            mark_cols.append(cols)
+
+        gather_mark(0)
+        load_vals(2)
+        key_words = sb.tile([P, I], U32, name="key_words", tag="window0", align_bytes=64)
+        nc.vector.tensor_copy(key_words[:], key_word_pool[:].bitcast(U32).indirect(offsets[:]))
+        load_vals(3)
+        gather_mark(1)
+
+        neg_lean = sb.tile([P, 1], F32, name="neg_lean")
+        nc.gpsimd.tensor_scalar(neg_lean[:], lean_col[:], -1.0, 0.0, ALU.mult, ALU.add)
+        neg_sharp = sb.tile([P, 1], F32, name="neg_sharp")
+        nc.gpsimd.tensor_scalar(neg_sharp[:], sharp_col[:], -1.0, 0.0, ALU.mult, ALU.add)
+
+        points = []
+        for c in range(CHUNKS):
+            cols = slice(P * c, P * (c + 1))
+            bank = ps.tile([P, 2 * Q], F32, name=f"points{c}")
+            nc.tensor.matmul_mx(
+                out=bank[:],
+                lhsT=key_words[:, cols].bitcast(FP8X4),
+                lhsT_scale=key_scales[:, cols],
+                rhs=q_codes[:].bitcast(FP8X4),
+                rhs_scale=q_scales[:],
+                start=True,
+                stop=True,
+            )
+            points.append(bank)
+        squares = [sb.tile([P, 2, Q], F32, name=f"squares{c}") for c in range(CHUNKS)]
+        for axis in range(2):
+            for c in range(CHUNKS):
+                nc.scalar.activation(
+                    squares[c][:, axis, :],
+                    points[c][:, Q * axis : Q * (axis + 1)],
+                    ACT.Square,
+                    bias=mark_cols[axis][:, c : c + 1],
+                    scale=-1.0,
+                )
+        dist = ps.tile([P, I], F32, name="dist", tag="rows")
+        for c in range(CHUNKS):
+            for axis in range(2):
+                nc.tensor.matmul(
+                    dist[:, P * c : P * (c + 1)],
+                    squares[c][:, axis, :],
+                    ident[:],
+                    start=(axis == 0),
+                    stop=(axis == 1),
+                    is_transpose=True,
+                )
+
+        v_codes = sb.tile([P, E], U32, name="v_codes", align_bytes=64)
+        v_scales = sb.tile([P, E], U8, name="v_scales", align_bytes=64)
+        v_grouped = {}
+
+        def gather_vals(j):
+            picked = sb.tile([P, I], BF16, name=f"v_picked{j}", tag=f"window{j + 1}", align_bytes=64)
+            nc.vector.tensor_copy(picked[:], val_pools[j][:].indirect(offsets[:]))
+            pairs = picked[:].bitcast(F32)
+            turned = ps.tile([P, 2, P], F32, name=f"v_turned{j}", tag=f"turn{j % 2}")
+            for u in range(2):
+                nc.tensor.transpose(turned[:, u, :], pairs[:, u : I // 2 : 2], ident[:])
+            v_grouped[j] = sb.tile([P, P * PACK], BF16, name=f"v_grouped{j}", align_bytes=64)
+            nc.scalar.copy(
+                v_grouped[j][:].bitcast(F32).rearrange("p (e u) -> p e u", u=2),
+                turned[:].rearrange("p u e -> p e u"),
+            )
+
+        def quantize_vals(j):
+            cols = slice(P * j, P * (j + 1))
+            nc.vector.quantize_mx(out=v_codes[:, cols].bitcast(FP8X4), scales=v_scales[:, cols], in_=v_grouped[j][:])
+
+        gather_vals(0)
+
+        cost = sb.tile([P, I], F32, name="cost")
+        cost_min = sb.tile([P, 1], F32, name="cost_min")
+        nc.vector.tensor_scalar(
+            cost[:].rearrange("q (t p) -> q t p", t=PACK),
+            dist[:].rearrange("q (p t) -> q t p", t=PACK),
+            lam_col[:],
+            None,
+            ALU.mult,
+            ALU.min,
+            accum_out=cost_min[:],
+        )
+        quantize_vals(0)
+        prob = sb.tile([P, I], F32, name="prob")
+        prob_sum = sb.tile([P, 1], F32, name="prob_sum")
+        nc.scalar.activation(prob[:], cost[:], ACT.Exp, bias=cost_min[:], scale=-1.0, accum_out=prob_sum[:])
+        slope = sb.tile([P, I], F32, name="slope")
+        nc.scalar.activation(slope[:], cost[:], ACT.Identity, bias=1.0, scale=neg_lean[:])
+        gather_vals(1)
+        inv_sum = sb.tile([P, 1], F32, name="inv_sum")
+        nc.vector.reciprocal(inv_sum[:], prob_sum[:])
+        share = sb.tile([P, I], F32, name="share")
+        nc.scalar.activation(share[:], prob[:], ACT.Copy, scale=inv_sum[:])
+        prob_cost = sb.tile([P, I], F32, name="prob_cost")
+        prob_cost_sum = sb.tile([P, 1], F32, name="prob_cost_sum")
+        nc.vector.scalar_tensor_tensor(
+            prob_cost[:], prob[:], 1.0, cost[:], ALU.mult, ALU.mult, accum_out=prob_cost_sum[:]
+        )
+        quantize_vals(1)
+        lift = sb.tile([P, 1], F32, name="lift")
+        nc.vector.tensor_scalar(lift[:], prob_cost_sum[:], lean_col[:], inv_sum[:], ALU.mult, ALU.mult)
+        weight = sb.tile([P, I], F32, name="weight")
+        nc.vector.scalar_tensor_tensor(weight[:], slope[:], lift[:], share[:], ALU.add, ALU.mult)
+
+        w_turned = ps.tile([P, PACK, Q], F32, name="w_turned", tag="rows")
+        for t in range(PACK):
+            nc.tensor.transpose(w_turned[:, t, :], weight[:, P * t : P * (t + 1)], ident[:])
+        gather_vals(2)
+        w_grouped = sb.tile([P, Q, PACK], BF16, name="w_grouped", align_bytes=64)
+        nc.vector.tensor_tensor(
+            w_grouped[:],
+            w_turned[:].rearrange("p t q -> p q t"),
+            os_cols[:].unsqueeze(1).to_broadcast([P, Q, PACK]),
+            ALU.mult,
+        )
+        quantize_vals(2)
+        w_codes = sb.tile([P, Q], U32, name="w_codes", align_bytes=64)
+        w_scales = sb.tile([P, Q], U8, name="w_scales", align_bytes=64)
+        nc.vector.quantize_mx(
+            out=w_codes[:].bitcast(FP8X4), scales=w_scales[:], in_=w_grouped[:].rearrange("p q t -> p (q t)")
+        )
+        gather_vals(3)
+        quantize_vals(3)
+
+        read = ps.tile([P, E], F32, name="read")
+        for j in range(PLANES):
+            cols = slice(P * j, P * (j + 1))
+            nc.tensor.matmul_mx(
+                out=read[:, cols],
+                lhsT=w_codes[:].bitcast(FP8X4),
+                lhsT_scale=w_scales[:],
+                rhs=v_codes[:, cols].bitcast(FP8X4),
+                rhs_scale=v_scales[:, cols],
+                start=True,
+                stop=True,
+            )
+        neg_logit = sb.tile([P, E], F32, name="neg_logit")
+        neg_max = sb.tile([P, 1], F32, name="neg_max")
+        nc.vector.tensor_scalar(neg_logit[:], read[:], neg_sharp[:], None, ALU.mult, ALU.min, accum_out=neg_max[:])
+        expo = sb.tile([P, E], F32, name="expo")
+        expo_sum = sb.tile([P, 1], F32, name="expo_sum")
+        nc.scalar.activation(expo[:], neg_logit[:], ACT.Exp, bias=neg_max[:], scale=-1.0, accum_out=expo_sum[:])
+        inv_expo_sum = sb.tile([P, 1], F32, name="inv_expo_sum")
+        nc.vector.reciprocal(inv_expo_sum[:], expo_sum[:])
+        result = sb.tile([P, E], F32, name="result")
+        nc.vector.tensor_scalar(result[:], expo[:], inv_expo_sum[:], float(E), ALU.mult, ALU.mult)
+        nc.sync.dma_start(out, result[:])

@@ -34,27 +34,25 @@ def tile_attend_maplace_leaning_readshares_kernel(
         offsets = sb.tile([P, I // 16], U16, name="offsets")
         nc.sync.dma_start(offsets[:], offs)
 
+        q_raw = []
+        for axis, src in enumerate((query, query2)):
+            raw = sb.tile([P, PACK, Q], F32, name=f"q_raw{axis}", tag=("slot_vals", "q_raw1")[axis], align_bytes=64)
+            nc.sync.dma_start(raw[:], src.rearrange("(p j) q -> p j q", j=PACK))
+            q_raw.append(raw)
+
         key_scale_pool = sb.tile([P, T], U8, name="key_scale_pool", tag="slot_scales", align_bytes=64)
         nc.vector.memset(key_scale_pool[:].bitcast(I32), 0)
         for quad in range(4):
-            nc.scalar.dma_start(
+            nc.sync.dma_start(
                 key_scale_pool[32 * quad : 32 * quad + 4, :].bitcast(I32),
                 keys_scales[0, 4 * quad : 4 * quad + 4, :].bitcast(I32),
             )
-        mark_pools = []
-        for axis, mark in enumerate((xmark, ymark)):
-            pool_tile = sb.tile([P, T], F32, name=f"mark_pool{axis}", tag=f"window{axis}", align_bytes=64)
-            nc.vector.memset(pool_tile[:].bitcast(I32), 0)
-            nc.scalar.dma_start(pool_tile[0:1, :], mark[0:1, :])
-            mark_pools.append(pool_tile)
-
-        q_raw = []
-        for axis, src in enumerate((query, query2)):
-            raw = sb.tile([P, PACK, Q], F32, name=f"q_raw{axis}")
-            nc.sync.dma_start(raw[:], src.rearrange("(p j) q -> p j q", j=PACK))
-            q_raw.append(raw)
         key_word_pool = sb.tile([P, T], I32, name="key_word_pool", tag="slot_keys", align_bytes=64)
         nc.sync.dma_start(key_word_pool[:], keys_words[0].rearrange("p n t -> p (n t)").bitcast(I32))
+        warm_in = sb.tile([P, 1], F32, name="warm_in")
+        nc.vector.memset(warm_in[:], 0.0)
+        warm = sb.tile([P, 1], F32, name="warm")
+        nc.scalar.activation(warm[:], warm_in[:], ACT.Exp)
 
         val_pools = {}
 
@@ -63,56 +61,62 @@ def tile_attend_maplace_leaning_readshares_kernel(
             val_pools[j] = sb.tile([P, T], F32, name=f"val_pool{j}", tag=tag, align_bytes=64)
             nc.sync.dma_start(val_pools[j][:], vals[P * j : P * (j + 1), :])
 
+        mark_pools = []
+
+        def load_mark(axis, mark):
+            pool_tile = sb.tile([P, T], F32, name=f"mark_pool{axis}", tag=f"window{axis}", align_bytes=64)
+            nc.vector.memset(pool_tile[:].bitcast(I32), 0)
+            nc.sync.dma_start(pool_tile[0:1, :], mark[0:1, :])
+            mark_pools.append(pool_tile)
+
+        load_mark(0, xmark)
+        q_grouped = sb.tile([P, 2, Q, PACK], BF16, name="q_grouped", tag="picked2", align_bytes=64)
+        for axis in range(2):
+            nc.scalar.copy(q_grouped[:, axis, :, :], q_raw[axis][:].rearrange("p j q -> p q j"))
         load_vals(0)
+        load_mark(1, ymark)
 
         ident = sb.tile([P, P], F32, name="ident")
         make_identity(nc, ident[:])
 
-        lam_col = sb.tile([P, 1], F32, name="lam_col")
-        lean_col = sb.tile([P, 1], F32, name="lean_col")
-        sharp_col = sb.tile([P, 1], F32, name="sharp_col")
-        os_cols = sb.tile([P, PACK], F32, name="os_cols")
-        nc.gpsimd.dma_start(lam_col[:], lam)
-        nc.gpsimd.dma_start(lean_col[:], lean)
-        nc.gpsimd.dma_start(os_cols[:], slot_factor[0].rearrange("(p t) -> p t", t=PACK))
-        nc.gpsimd.dma_start(sharp_col[:], vsharp)
-
-        q_grouped = sb.tile([P, 2, Q, PACK], BF16, name="q_grouped", align_bytes=64)
-        for axis in range(2):
-            nc.scalar.copy(q_grouped[:, axis, :, :], q_raw[axis][:].rearrange("p j q -> p q j"))
+        key_scales = sb.tile([P, I], U8, name="key_scales", align_bytes=64)
+        nc.vector.tensor_copy(key_scales[:], key_scale_pool[:].indirect(offsets[:]))
+        lean_col = sb.tile([P, 1], F32, name="lean_col", tag="q_raw1", align_bytes=64)
+        nc.sync.dma_start(lean_col[:], lean)
+        load_vals(1)
         q_codes = sb.tile([P, 2 * Q], U32, name="q_codes", align_bytes=64)
         q_scales = sb.tile([P, 2 * Q], U8, name="q_scales", align_bytes=64)
 
-        key_scales = sb.tile([P, I], U8, name="key_scales", align_bytes=64)
-        nc.vector.tensor_copy(key_scales[:], key_scale_pool[:].indirect(offsets[:]))
-        load_vals(1)
         nc.vector.quantize_mx(
             out=q_codes[:].bitcast(FP8X4), scales=q_scales[:], in_=q_grouped[:].rearrange("p a q j -> p (a q j)")
         )
+        lam_col = sb.tile([P, 1], F32, name="lam_col", tag="picked2", align_bytes=64)
+        nc.sync.dma_start(lam_col[:], lam)
+
 
         mark_cols = []
 
-        def gather_mark(axis):
+        def gather_mark(axis, banks):
             row = sb.tile([P, I], F32, name=f"mark_row{axis}", tag=f"row{axis}", align_bytes=64)
-            nc.vector.tensor_copy(row[:], mark_pools[axis][:].indirect(offsets[:]))
-            turned = ps.tile([P, CHUNKS, P], F32, name=f"mark_turned{axis}", tag=f"turn{axis}")
-            for c in range(CHUNKS):
-                nc.tensor.transpose(turned[:, c, :], row[:, P * c : P * (c + 1)], ident[:])
-            cols = sb.tile([P, CHUNKS], F32, name=f"mark_cols{axis}")
-            nc.scalar.copy(cols[:], turned[:, :, 0])
-            mark_cols.append(cols)
+            per = CHUNKS // len(banks)
+            for part, bank in enumerate(banks):
+                nc.vector.tensor_copy(
+                    row[:, P * per * part : P * per * (part + 1)],
+                    mark_pools[axis][:].indirect(offsets[:, 8 * per * part : 8 * per * (part + 1)]),
+                )
+                turned = ps.tile([P, per, P], F32, name=f"mark_turned{axis}_{part}", tag=bank)
+                for k in range(per):
+                    c = per * part + k
+                    nc.tensor.transpose(turned[:, k, :], row[:, P * c : P * (c + 1)], ident[:])
+                cols = sb.tile([P, per], F32, name=f"mark_cols{axis}_{part}")
+                nc.scalar.copy(cols[:], turned[:, :, 0])
+                mark_cols.extend([cols[:, k : k + 1] for k in range(per)])
 
-        gather_mark(0)
-        load_vals(2)
+        gather_mark(0, ("turn0",))
         key_words = sb.tile([P, I], U32, name="key_words", tag="window0", align_bytes=64)
         nc.vector.tensor_copy(key_words[:], key_word_pool[:].bitcast(U32).indirect(offsets[:]))
+        load_vals(2)
         load_vals(3)
-        gather_mark(1)
-
-        neg_lean = sb.tile([P, 1], F32, name="neg_lean")
-        nc.gpsimd.tensor_scalar(neg_lean[:], lean_col[:], -1.0, 0.0, ALU.mult, ALU.add)
-        neg_sharp = sb.tile([P, 1], F32, name="neg_sharp")
-        nc.gpsimd.tensor_scalar(neg_sharp[:], sharp_col[:], -1.0, 0.0, ALU.mult, ALU.add)
 
         points = []
         for c in range(CHUNKS):
@@ -128,6 +132,11 @@ def tile_attend_maplace_leaning_readshares_kernel(
                 stop=True,
             )
             points.append(bank)
+        gather_mark(1, ("turn1", "turn2"))
+        os_cols = sb.tile([P, PACK], F32, name="os_cols", tag="row1", align_bytes=64)
+        nc.sync.dma_start(os_cols[:], slot_factor[0].rearrange("(p t) -> p t", t=PACK))
+        sharp_col = sb.tile([P, 1], F32, name="sharp_col", tag="window0", align_bytes=64)
+        nc.sync.dma_start(sharp_col[:], vsharp)
         squares = [sb.tile([P, 2, Q], F32, name=f"squares{c}") for c in range(CHUNKS)]
         for axis in range(2):
             for c in range(CHUNKS):
@@ -135,45 +144,53 @@ def tile_attend_maplace_leaning_readshares_kernel(
                     squares[c][:, axis, :],
                     points[c][:, Q * axis : Q * (axis + 1)],
                     ACT.Square,
-                    bias=mark_cols[axis][:, c : c + 1],
+                    bias=mark_cols[CHUNKS * axis + c],
                     scale=-1.0,
                 )
         dist = ps.tile([P, I], F32, name="dist", tag="rows")
-        for c in range(CHUNKS):
-            for axis in range(2):
+        for axis in range(2):
+            for c in range(CHUNKS):
                 nc.tensor.matmul(
                     dist[:, P * c : P * (c + 1)],
                     squares[c][:, axis, :],
                     ident[:],
-                    start=(axis == 0),
-                    stop=(axis == 1),
+                    start=(axis == 0 and c == 0),
+                    stop=(axis == 1 and c == CHUNKS - 1),
                     is_transpose=True,
                 )
 
-        v_codes = sb.tile([P, E], U32, name="v_codes", align_bytes=64)
-        v_scales = sb.tile([P, E], U8, name="v_scales", align_bytes=64)
-        v_grouped = {}
+        v_grouped = [sb.tile([P, 2, P * PACK], BF16, name="v_grouped0", align_bytes=64)]
+
+        v_picked = {}
 
         def gather_vals(j):
-            picked = sb.tile([P, I], BF16, name=f"v_picked{j}", tag=f"window{j + 1}", align_bytes=64)
+            picked = sb.tile([P, I], BF16, name=f"v_picked{j}", tag=("window1", "picked1", "picked2", "picked3")[j], align_bytes=64)
             nc.vector.tensor_copy(picked[:], val_pools[j][:].indirect(offsets[:]))
-            pairs = picked[:].bitcast(F32)
-            turned = ps.tile([P, 2, P], F32, name=f"v_turned{j}", tag=f"turn{j % 2}")
+            v_picked[j] = picked
+
+        def turn_vals(j):
+            pairs = v_picked[j][:].bitcast(F32)
+            turned = ps.tile([P, 2, P], F32, name=f"v_turned{j}", tag=("turn0", "rows", "turn0", "turn1")[j])
             for u in range(2):
                 nc.tensor.transpose(turned[:, u, :], pairs[:, u : I // 2 : 2], ident[:])
-            v_grouped[j] = sb.tile([P, P * PACK], BF16, name=f"v_grouped{j}", align_bytes=64)
             nc.scalar.copy(
-                v_grouped[j][:].bitcast(F32).rearrange("p (e u) -> p e u", u=2),
+                v_grouped[j // 2][:, j % 2, :].bitcast(F32).rearrange("p (e u) -> p e u", u=2),
                 turned[:].rearrange("p u e -> p e u"),
             )
 
-        def quantize_vals(j):
-            cols = slice(P * j, P * (j + 1))
-            nc.vector.quantize_mx(out=v_codes[:, cols].bitcast(FP8X4), scales=v_scales[:, cols], in_=v_grouped[j][:])
+        def quantize_vals(h, tag):
+            codes = sb.tile([P, E // 2], U32, name=f"v_codes{h}", tag=tag, align_bytes=64)
+            scales = sb.tile([P, E // 2], U8, name=f"v_scales{h}", align_bytes=64)
+            nc.vector.quantize_mx(
+                out=codes[:].bitcast(FP8X4), scales=scales[:], in_=v_grouped[h][:].rearrange("p j x -> p (j x)")
+            )
+            return codes, scales
 
         gather_vals(0)
+        turn_vals(0)
+        gather_vals(1)
 
-        cost = sb.tile([P, I], F32, name="cost")
+        cost = sb.tile([P, I], F32, name="cost", tag="slot_scales", align_bytes=64)
         cost_min = sb.tile([P, 1], F32, name="cost_min")
         nc.vector.tensor_scalar(
             cost[:].rearrange("q (t p) -> q t p", t=PACK),
@@ -184,68 +201,80 @@ def tile_attend_maplace_leaning_readshares_kernel(
             ALU.min,
             accum_out=cost_min[:],
         )
-        quantize_vals(0)
-        prob = sb.tile([P, I], F32, name="prob")
+        prob = sb.tile([P, I], F32, name="prob", tag="prob", align_bytes=64)
         prob_sum = sb.tile([P, 1], F32, name="prob_sum")
         nc.scalar.activation(prob[:], cost[:], ACT.Exp, bias=cost_min[:], scale=-1.0, accum_out=prob_sum[:])
-        slope = sb.tile([P, I], F32, name="slope")
-        nc.scalar.activation(slope[:], cost[:], ACT.Identity, bias=1.0, scale=neg_lean[:])
-        gather_vals(1)
-        inv_sum = sb.tile([P, 1], F32, name="inv_sum")
-        nc.vector.reciprocal(inv_sum[:], prob_sum[:])
+        neg_slope = sb.tile([P, I], F32, name="neg_slope", tag="picked3", align_bytes=64)
+        nc.scalar.activation(neg_slope[:], cost[:], ACT.Copy, bias=-1.0, scale=lean_col[:])
+        turn_vals(1)
+        gather_vals(2)
+        after_exp = sb.tile([P, I + 8], F32, name="after_exp", tag="row0", align_bytes=64)
+        inv_sum = after_exp[:, I : I + 1]
+        nc.vector.reciprocal(inv_sum, prob_sum[:])
         share = sb.tile([P, I], F32, name="share")
-        nc.scalar.activation(share[:], prob[:], ACT.Copy, scale=inv_sum[:])
-        prob_cost = sb.tile([P, I], F32, name="prob_cost")
+        nc.scalar.activation(share[:], prob[:], ACT.Copy, scale=inv_sum)
         prob_cost_sum = sb.tile([P, 1], F32, name="prob_cost_sum")
         nc.vector.scalar_tensor_tensor(
-            prob_cost[:], prob[:], 1.0, cost[:], ALU.mult, ALU.mult, accum_out=prob_cost_sum[:]
+            after_exp[:, 0:I], prob[:], 1.0, cost[:], ALU.mult, ALU.mult, accum_out=prob_cost_sum[:]
         )
-        quantize_vals(1)
+        v_grouped.append(sb.tile([P, 2, P * PACK], BF16, name="v_grouped1", tag="prob", align_bytes=64))
+        turn_vals(2)
+        v_quant = [quantize_vals(0, "picked2")]
         lift = sb.tile([P, 1], F32, name="lift")
-        nc.vector.tensor_scalar(lift[:], prob_cost_sum[:], lean_col[:], inv_sum[:], ALU.mult, ALU.mult)
-        weight = sb.tile([P, I], F32, name="weight")
-        nc.vector.scalar_tensor_tensor(weight[:], slope[:], lift[:], share[:], ALU.add, ALU.mult)
+        nc.vector.tensor_scalar(lift[:], prob_cost_sum[:], lean_col[:], inv_sum, ALU.mult, ALU.mult)
+        neg_weight = sb.tile([P, I], F32, name="neg_weight")
+        nc.vector.scalar_tensor_tensor(neg_weight[:], neg_slope[:], lift[:], share[:], ALU.subtract, ALU.mult)
 
-        w_turned = ps.tile([P, PACK, Q], F32, name="w_turned", tag="rows")
+        w_turned = ps.tile([P, PACK, Q], F32, name="w_turned", tag="points2")
         for t in range(PACK):
-            nc.tensor.transpose(w_turned[:, t, :], weight[:, P * t : P * (t + 1)], ident[:])
-        gather_vals(2)
-        w_grouped = sb.tile([P, Q, PACK], BF16, name="w_grouped", align_bytes=64)
+            nc.tensor.transpose(w_turned[:, t, :], neg_weight[:, P * t : P * (t + 1)], ident[:])
+        gather_vals(3)
+        turn_vals(3)
+        w_grouped = sb.tile([P, Q, PACK], BF16, name="w_grouped", tag="slot_keys", align_bytes=64)
         nc.vector.tensor_tensor(
             w_grouped[:],
             w_turned[:].rearrange("p t q -> p q t"),
             os_cols[:].unsqueeze(1).to_broadcast([P, Q, PACK]),
             ALU.mult,
         )
-        quantize_vals(2)
         w_codes = sb.tile([P, Q], U32, name="w_codes", align_bytes=64)
         w_scales = sb.tile([P, Q], U8, name="w_scales", align_bytes=64)
         nc.vector.quantize_mx(
             out=w_codes[:].bitcast(FP8X4), scales=w_scales[:], in_=w_grouped[:].rearrange("p q t -> p (q t)")
         )
-        gather_vals(3)
-        quantize_vals(3)
 
-        read = ps.tile([P, E], F32, name="read")
-        for j in range(PLANES):
-            cols = slice(P * j, P * (j + 1))
+        v_quant.append(quantize_vals(1, "slot_keys"))
+
+        neg_logit = sb.tile([P, E], F32, name="neg_logit")
+        neg_max = [sb.tile([P, 1], F32, name=f"neg_max{h}") for h in range(2)]
+        for h in range(2):
+            cols = slice(E // 2 * h, E // 2 * (h + 1))
+            read = ps.tile([P, E // 2], F32, name=f"read{h}", tag=f"points{h}")
             nc.tensor.matmul_mx(
-                out=read[:, cols],
+                out=read[:],
                 lhsT=w_codes[:].bitcast(FP8X4),
                 lhsT_scale=w_scales[:],
-                rhs=v_codes[:, cols].bitcast(FP8X4),
-                rhs_scale=v_scales[:, cols],
+                rhs=v_quant[h][0][:].bitcast(FP8X4),
+                rhs_scale=v_quant[h][1][:],
                 start=True,
                 stop=True,
             )
-        neg_logit = sb.tile([P, E], F32, name="neg_logit")
-        neg_max = sb.tile([P, 1], F32, name="neg_max")
-        nc.vector.tensor_scalar(neg_logit[:], read[:], neg_sharp[:], None, ALU.mult, ALU.min, accum_out=neg_max[:])
+            nc.vector.tensor_scalar(
+                neg_logit[:, cols],
+                read[:],
+                sharp_col[:],
+                neg_max[0][:] if h else None,
+                ALU.mult,
+                ALU.min,
+                accum_out=neg_max[h][:],
+            )
         expo = sb.tile([P, E], F32, name="expo")
         expo_sum = sb.tile([P, 1], F32, name="expo_sum")
-        nc.scalar.activation(expo[:], neg_logit[:], ACT.Exp, bias=neg_max[:], scale=-1.0, accum_out=expo_sum[:])
+        nc.scalar.activation(expo[:], neg_logit[:], ACT.Exp, bias=neg_max[1][:], scale=-1.0, accum_out=expo_sum[:])
         inv_expo_sum = sb.tile([P, 1], F32, name="inv_expo_sum")
         nc.vector.reciprocal(inv_expo_sum[:], expo_sum[:])
-        result = sb.tile([P, E], F32, name="result")
-        nc.vector.tensor_scalar(result[:], expo[:], inv_expo_sum[:], float(E), ALU.mult, ALU.mult)
-        nc.sync.dma_start(out, result[:])
+        for h, queue in enumerate((nc.sync, nc.scalar)):
+            cols = slice(E // 2 * h, E // 2 * (h + 1))
+            result = sb.tile([P, E // 2], F32, name=f"result{h}")
+            nc.vector.tensor_scalar(result[:], expo[:, cols], inv_expo_sum[:], float(E), ALU.mult, ALU.mult)
+            queue.dma_start(out[:, cols], result[:])

from contextlib import ExitStack

import concourse.mybir as mybir
from concourse.masks import make_identity

D, T, I, Q, E = 512, 2048, 512, 128, 512
FLOPS = 2 * D * I * 2 * Q + 2 * I * Q * E
BYTES = 4 * (2 * D * Q + E * T + 2 * T + 3 * Q + I + Q * E) + D * T + 16 * T + 2 * 128 * 32

F32 = mybir.dt.float32
BF16 = mybir.dt.bfloat16
I32 = mybir.dt.int32
U32 = mybir.dt.uint32
U16 = mybir.dt.uint16
U8 = mybir.dt.uint8
FP8X4 = mybir.dt.float8_e4m3fn_x4
ALU = mybir.AluOpType
ACT = mybir.ActivationFunctionType

P = 128
PACK = 4
CHUNKS = I // P
PLANES = E // P


def tile_attend_maplace_leaning_readshares_kernel(
    tc, query, query2, keys_words, keys_scales, xmark, ymark, lam, lean, slot_factor, vals, vsharp, offs, out
):
    nc = tc.nc
    with ExitStack() as ctx:
        sb = ctx.enter_context(tc.tile_pool(name="sb", bufs=1))
        ps = ctx.enter_context(tc.psum_pool(name="ps", bufs=1))

        offsets = sb.tile([P, I // 16], U16, name="offsets")
        nc.sync.dma_start(offsets[:], offs)

        q_raw = []
        for axis, src in enumerate((query, query2)):
            raw = sb.tile([P, PACK, Q], F32, name=f"q_raw{axis}", tag=("slot_vals", "q_raw1")[axis], align_bytes=64)
            nc.sync.dma_start(raw[:], src.rearrange("(p j) q -> p j q", j=PACK))
            q_raw.append(raw)

        key_scale_pool = sb.tile([P, T], U8, name="key_scale_pool", tag="slot_scales", align_bytes=64)
        nc.vector.memset(key_scale_pool[:].bitcast(I32), 0)
        for quad in range(4):
            nc.sync.dma_start(
                key_scale_pool[32 * quad : 32 * quad + 4, :].bitcast(I32),
                keys_scales[0, 4 * quad : 4 * quad + 4, :].bitcast(I32),
            )
        key_word_pool = sb.tile([P, T], I32, name="key_word_pool", tag="slot_keys", align_bytes=64)
        nc.sync.dma_start(key_word_pool[:], keys_words[0].rearrange("p n t -> p (n t)").bitcast(I32))
        warm_in = sb.tile([P, 1], F32, name="warm_in")
        nc.vector.memset(warm_in[:], 0.0)
        warm = sb.tile([P, 1], F32, name="warm")
        nc.scalar.activation(warm[:], warm_in[:], ACT.Exp)

        val_pools = {}

        def load_vals(j):
            tag = ("slot_vals", "slot_scales", "row0", "slot_keys")[j]
            val_pools[j] = sb.tile([P, T], F32, name=f"val_pool{j}", tag=tag, align_bytes=64)
            nc.sync.dma_start(val_pools[j][:], vals[P * j : P * (j + 1), :])

        mark_pools = []

        def load_mark(axis, mark):
            pool_tile = sb.tile([P, T], F32, name=f"mark_pool{axis}", tag=f"window{axis}", align_bytes=64)
            nc.vector.memset(pool_tile[:].bitcast(I32), 0)
            nc.sync.dma_start(pool_tile[0:1, :], mark[0:1, :])
            mark_pools.append(pool_tile)

        load_mark(0, xmark)
        q_grouped = sb.tile([P, 2, Q, PACK], BF16, name="q_grouped", tag="picked2", align_bytes=64)
        for axis in range(2):
            nc.scalar.copy(q_grouped[:, axis, :, :], q_raw[axis][:].rearrange("p j q -> p q j"))
        load_vals(0)
        load_mark(1, ymark)

        ident = sb.tile([P, P], F32, name="ident")
        make_identity(nc, ident[:])

        key_scales = sb.tile([P, I], U8, name="key_scales", align_bytes=64)
        nc.vector.tensor_copy(key_scales[:], key_scale_pool[:].indirect(offsets[:]))
        lean_col = sb.tile([P, 1], F32, name="lean_col", tag="q_raw1", align_bytes=64)
        nc.sync.dma_start(lean_col[:], lean)
        load_vals(1)
        q_codes = sb.tile([P, 2 * Q], U32, name="q_codes", align_bytes=64)
        q_scales = sb.tile([P, 2 * Q], U8, name="q_scales", align_bytes=64)

        nc.vector.quantize_mx(
            out=q_codes[:].bitcast(FP8X4), scales=q_scales[:], in_=q_grouped[:].rearrange("p a q j -> p (a q j)")
        )
        lam_col = sb.tile([P, 1], F32, name="lam_col", tag="picked2", align_bytes=64)
        nc.sync.dma_start(lam_col[:], lam)


        mark_cols = []

        def gather_mark(axis, banks):
            row = sb.tile([P, I], F32, name=f"mark_row{axis}", tag=f"row{axis}", align_bytes=64)
            per = CHUNKS // len(banks)
            for part, bank in enumerate(banks):
                nc.vector.tensor_copy(
                    row[:, P * per * part : P * per * (part + 1)],
                    mark_pools[axis][:].indirect(offsets[:, 8 * per * part : 8 * per * (part + 1)]),
                )
                turned = ps.tile([P, per, P], F32, name=f"mark_turned{axis}_{part}", tag=bank)
                for k in range(per):
                    c = per * part + k
                    nc.tensor.transpose(turned[:, k, :], row[:, P * c : P * (c + 1)], ident[:])
                cols = sb.tile([P, per], F32, name=f"mark_cols{axis}_{part}")
                nc.scalar.copy(cols[:], turned[:, :, 0])
                mark_cols.extend([cols[:, k : k + 1] for k in range(per)])

        gather_mark(0, ("turn0",))
        key_words = sb.tile([P, I], U32, name="key_words", tag="window0", align_bytes=64)
        nc.vector.tensor_copy(key_words[:], key_word_pool[:].bitcast(U32).indirect(offsets[:]))
        load_vals(2)
        load_vals(3)

        points = []
        for c in range(CHUNKS):
            cols = slice(P * c, P * (c + 1))
            bank = ps.tile([P, 2 * Q], F32, name=f"points{c}")
            nc.tensor.matmul_mx(
                out=bank[:],
                lhsT=key_words[:, cols].bitcast(FP8X4),
                lhsT_scale=key_scales[:, cols],
                rhs=q_codes[:].bitcast(FP8X4),
                rhs_scale=q_scales[:],
                start=True,
                stop=True,
            )
            points.append(bank)
        gather_mark(1, ("turn1", "turn2"))
        os_cols = sb.tile([P, PACK], F32, name="os_cols", tag="row1", align_bytes=64)
        nc.sync.dma_start(os_cols[:], slot_factor[0].rearrange("(p t) -> p t", t=PACK))
        sharp_col = sb.tile([P, 1], F32, name="sharp_col", tag="window0", align_bytes=64)
        nc.sync.dma_start(sharp_col[:], vsharp)
        squares = [sb.tile([P, 2, Q], F32, name=f"squares{c}") for c in range(CHUNKS)]
        for axis in range(2):
            for c in range(CHUNKS):
                nc.scalar.activation(
                    squares[c][:, axis, :],
                    points[c][:, Q * axis : Q * (axis + 1)],
                    ACT.Square,
                    bias=mark_cols[CHUNKS * axis + c],
                    scale=-1.0,
                )
        dist = ps.tile([P, I], F32, name="dist", tag="rows")
        for axis in range(2):
            for c in range(CHUNKS):
                nc.tensor.matmul(
                    dist[:, P * c : P * (c + 1)],
                    squares[c][:, axis, :],
                    ident[:],
                    start=(axis == 0 and c == 0),
                    stop=(axis == 1 and c == CHUNKS - 1),
                    is_transpose=True,
                )

        v_grouped = [sb.tile([P, 2, P * PACK], BF16, name="v_grouped0", align_bytes=64)]

        v_picked = {}

        def gather_vals(j):
            picked = sb.tile([P, I], BF16, name=f"v_picked{j}", tag=("window1", "picked1", "picked2", "picked3")[j], align_bytes=64)
            nc.vector.tensor_copy(picked[:], val_pools[j][:].indirect(offsets[:]))
            v_picked[j] = picked

        def turn_vals(j):
            pairs = v_picked[j][:].bitcast(F32)
            turned = ps.tile([P, 2, P], F32, name=f"v_turned{j}", tag=("turn0", "rows", "turn0", "turn1")[j])
            for u in range(2):
                nc.tensor.transpose(turned[:, u, :], pairs[:, u : I // 2 : 2], ident[:])
            nc.scalar.copy(
                v_grouped[j // 2][:, j % 2, :].bitcast(F32).rearrange("p (e u) -> p e u", u=2),
                turned[:].rearrange("p u e -> p e u"),
            )

        def quantize_vals(h, tag):
            codes = sb.tile([P, E // 2], U32, name=f"v_codes{h}", tag=tag, align_bytes=64)
            scales = sb.tile([P, E // 2], U8, name=f"v_scales{h}", align_bytes=64)
            nc.vector.quantize_mx(
                out=codes[:].bitcast(FP8X4), scales=scales[:], in_=v_grouped[h][:].rearrange("p j x -> p (j x)")
            )
            return codes, scales

        gather_vals(0)
        turn_vals(0)
        gather_vals(1)

        cost = sb.tile([P, I], F32, name="cost", tag="slot_scales", align_bytes=64)
        cost_min = sb.tile([P, 1], F32, name="cost_min")
        nc.vector.tensor_scalar(
            cost[:].rearrange("q (t p) -> q t p", t=PACK),
            dist[:].rearrange("q (p t) -> q t p", t=PACK),
            lam_col[:],
            None,
            ALU.mult,
            ALU.min,
            accum_out=cost_min[:],
        )
        prob = sb.tile([P, I], F32, name="prob", tag="prob", align_bytes=64)
        prob_sum = sb.tile([P, 1], F32, name="prob_sum")
        nc.scalar.activation(prob[:], cost[:], ACT.Exp, bias=cost_min[:], scale=-1.0, accum_out=prob_sum[:])
        neg_slope = sb.tile([P, I], F32, name="neg_slope", tag="picked3", align_bytes=64)
        nc.scalar.activation(neg_slope[:], cost[:], ACT.Copy, bias=-1.0, scale=lean_col[:])
        turn_vals(1)
        gather_vals(2)
        after_exp = sb.tile([P, I + 8], F32, name="after_exp", tag="row0", align_bytes=64)
        inv_sum = after_exp[:, I : I + 1]
        nc.vector.reciprocal(inv_sum, prob_sum[:])
        share = sb.tile([P, I], F32, name="share")
        nc.scalar.activation(share[:], prob[:], ACT.Copy, scale=inv_sum)
        prob_cost_sum = sb.tile([P, 1], F32, name="prob_cost_sum")
        nc.vector.scalar_tensor_tensor(
            after_exp[:, 0:I], prob[:], 1.0, cost[:], ALU.mult, ALU.mult, accum_out=prob_cost_sum[:]
        )
        v_grouped.append(sb.tile([P, 2, P * PACK], BF16, name="v_grouped1", tag="prob", align_bytes=64))
        turn_vals(2)
        v_quant = [quantize_vals(0, "picked2")]
        lift = sb.tile([P, 1], F32, name="lift")
        nc.vector.tensor_scalar(lift[:], prob_cost_sum[:], lean_col[:], inv_sum, ALU.mult, ALU.mult)
        neg_weight = sb.tile([P, I], F32, name="neg_weight")
        nc.vector.scalar_tensor_tensor(neg_weight[:], neg_slope[:], lift[:], share[:], ALU.subtract, ALU.mult)

        w_turned = ps.tile([P, PACK, Q], F32, name="w_turned", tag="points2")
        for t in range(PACK):
            nc.tensor.transpose(w_turned[:, t, :], neg_weight[:, P * t : P * (t + 1)], ident[:])
        gather_vals(3)
        turn_vals(3)
        w_grouped = sb.tile([P, Q, PACK], BF16, name="w_grouped", tag="slot_keys", align_bytes=64)
        nc.vector.tensor_tensor(
            w_grouped[:],
            w_turned[:].rearrange("p t q -> p q t"),
            os_cols[:].unsqueeze(1).to_broadcast([P, Q, PACK]),
            ALU.mult,
        )
        w_codes = sb.tile([P, Q], U32, name="w_codes", align_bytes=64)
        w_scales = sb.tile([P, Q], U8, name="w_scales", align_bytes=64)
        nc.vector.quantize_mx(
            out=w_codes[:].bitcast(FP8X4), scales=w_scales[:], in_=w_grouped[:].rearrange("p q t -> p (q t)")
        )

        v_quant.append(quantize_vals(1, "slot_keys"))

        neg_logit = sb.tile([P, E], F32, name="neg_logit")
        neg_max = [sb.tile([P, 1], F32, name=f"neg_max{h}") for h in range(2)]
        for h in range(2):
            cols = slice(E // 2 * h, E // 2 * (h + 1))
            read = ps.tile([P, E // 2], F32, name=f"read{h}", tag=f"points{h}")
            nc.tensor.matmul_mx(
                out=read[:],
                lhsT=w_codes[:].bitcast(FP8X4),
                lhsT_scale=w_scales[:],
                rhs=v_quant[h][0][:].bitcast(FP8X4),
                rhs_scale=v_quant[h][1][:],
                start=True,
                stop=True,
            )
            nc.vector.tensor_scalar(
                neg_logit[:, cols],
                read[:],
                sharp_col[:],
                neg_max[0][:] if h else None,
                ALU.mult,
                ALU.min,
                accum_out=neg_max[h][:],
            )
        expo = sb.tile([P, E], F32, name="expo")
        expo_sum = sb.tile([P, 1], F32, name="expo_sum")
        nc.scalar.activation(expo[:], neg_logit[:], ACT.Exp, bias=neg_max[1][:], scale=-1.0, accum_out=expo_sum[:])
        inv_expo_sum = sb.tile([P, 1], F32, name="inv_expo_sum")
        nc.vector.reciprocal(inv_expo_sum[:], expo_sum[:])
        for h, queue in enumerate((nc.sync, nc.scalar)):
            cols = slice(E // 2 * h, E // 2 * (h + 1))
            result = sb.tile([P, E // 2], F32, name=f"result{h}")
            nc.vector.tensor_scalar(result[:], expo[:, cols], inv_expo_sum[:], float(E), ALU.mult, ALU.mult)
            queue.dma_start(out[:, cols], result[:])
